import numpy as np
import ml_dtypes


def mxq(x, axis, fmt="e4m3"):
    dtype, down = {"e4m3": (ml_dtypes.float8_e4m3fn, 7), "e5m2": (ml_dtypes.float8_e5m2, 14)}[fmt]
    v = np.moveaxis(np.asarray(x, np.float32).astype(ml_dtypes.bfloat16).astype(np.float64), axis, -1)
    blocks = v.reshape(v.shape[:-1] + (-1, 32))
    amax = np.abs(blocks).max(-1, keepdims=True)
    byte = np.maximum(np.where(amax > 0, np.frexp(amax)[1] - 1 + 127, 0) - down, 1)
    scale = np.exp2(byte - 127.0)
    codes = (blocks / scale).astype(np.float32).astype(dtype).astype(np.float64)
    return np.moveaxis((codes * scale).reshape(v.shape), -1, axis)


WIDE = False


def mx_kscale(k, group=512):
    if not WIDE:
        return np.ones(k)
    levels = np.array([10, -10, 5, -5, 0])
    if group != 512:
        return np.exp2(np.random.permutation(np.resize(levels, k // group))).repeat(group)
    if k % 512:
        return np.exp2(np.random.permutation(np.resize(levels, k // 32))).repeat(32)
    a = np.empty((k // 512, 16))
    for p in range(k // 512):
        a[p, :8] = np.random.permutation(np.resize(levels, 8))
        for g in range(8):
            far = levels[np.abs(levels - a[p, g]) >= 10]
            a[p, g + 8] = far[np.random.randint(len(far))]
    return np.exp2(a.ravel()).repeat(32)


def f64(x):
    return np.asarray(x).astype(np.float64)


def gelu(v):
    return 0.5 * v * (1.0 + np.tanh(0.7978845608028654 * (v + 0.044715 * v ** 3)))


K, R, M, N = 1024, 256, 512, 512


def setup_inputs():
    n = np.random.standard_normal
    s = mx_kscale(K)[:, None]
    z = mx_kscale(R, 0)
    return {
        "x": (n((K, N)) * s).astype(np.float32),
        "w": (n((K, M)) / np.sqrt(K) / s).astype(np.float32),
        "a": (n((K, R)) / np.sqrt(K) / s * z).astype(np.float32),
        "bb": (n((R, M)) / np.sqrt(R) / z[:, None]).astype(np.float32),
    }


def reference(x, w, a, bb):
    xq = mxq(f64(x), 0, "e4m3")
    z = mxq(f64(a), 0, "e4m3").T @ xq
    y = (mxq(f64(w), 0, "e4m3").T @ xq) + (mxq(f64(bb), 0, "e4m3").T @ mxq(z, 0, "e4m3"))
    y = gelu(y)
    return y

@@ -1,0 +1,267 @@
+from contextlib import ExitStack
+
+import concourse.mybir as mybir
+
+K, R, M, N = 1024, 256, 512, 512
+FLOPS = 2 * N * (K * R + K * M + R * M)
+
+F32 = mybir.dt.float32
+BF16 = mybir.dt.bfloat16
+I32 = mybir.dt.int32
+U8 = mybir.dt.uint8
+FP8X4 = mybir.dt.float8_e4m3fn_x4
+GELU = mybir.ActivationFunctionType.Gelu_apprx_tanh
+ADD = mybir.AluOpType.add
+
+P = 128
+HALF = 64
+PACK = 4
+T = 128
+PASS = P * PACK
+A_WORDS = 8 * HALF
+B_WORDS = 2 * T
+
+
+def tile_rows_lora_gelu_kernel(tc, x, w, a, bb, out):
+    nc = tc.nc
+    with ExitStack() as ctx:
+        sb = ctx.enter_context(tc.tile_pool(name="sb", bufs=1))
+        ps = ctx.enter_context(tc.psum_pool(name="ps", bufs=1))
+        ctx.enter_context(tc.manual_schedule())
+
+        def sbuf(name, shape, dtype):
+            return sb.tile(shape, dtype, name=name, align_bytes=64)
+
+        def load(name, src, c, c0, c1):
+            raw = sbuf(name, [P, PACK, c1 - c0], F32)
+            rows = src[c * PASS : (c + 1) * PASS, c0:c1]
+            nc.sync.dma_start(out=raw[:], in_=rows.rearrange("(p j) n -> p j n", j=PACK))
+            return raw
+
+        def copy(engine, dst, src):
+            if engine == "vector":
+                nc.vector.tensor_copy(out=dst, in_=src)
+            else:
+                nc.scalar.copy(out=dst, in_=src)
+
+        def interleave(engine, packed, raw, c0, c1):
+            dst = packed[:, PACK * c0 : PACK * c1].rearrange("p (c i j) -> p c j i", i=4, j=PACK)
+            src = raw[:, :, c0:c1].rearrange("p j (c i) -> p c j i", i=4)
+            copy(engine, dst, src)
+
+        def deal(engine, packed, raw, m0, m1):
+            dst = packed[:].rearrange("p (s m j) -> p m j s", s=PACK, j=PACK)[:, m0:m1]
+            src = raw[:].rearrange("p j (m s) -> p m j s", s=PACK)[:, m0:m1]
+            copy(engine, dst, src)
+
+        def operand(name, words):
+            both = sbuf(name, [P, words + words // 4], I32)
+            return both, both[:, 0:words].bitcast(FP8X4), both[:, words:].bitcast(U8)
+
+        def quantize(op, w0, packed, c0, c1):
+            nc.vector.quantize_mx(
+                out=op[1][:, w0 : w0 + c1 - c0],
+                scales=op[2][:, w0 : w0 + c1 - c0],
+                in_=packed[:, PACK * c0 : PACK * c1],
+            )
+
+        def product(dst, lhs, l0, rhs, r0, rows, start, stop):
+            nc.tensor.matmul_mx(
+                out=dst,
+                lhsT=lhs[1][rows, l0 : l0 + T],
+                lhsT_scale=lhs[2][rows, l0 : l0 + T],
+                rhs=rhs[1][rows, r0 : r0 + T],
+                rhs_scale=rhs[2][rows, r0 : r0 + T],
+                start=start,
+                stop=stop,
+            )
+
+        whole = slice(0, P)
+        halves = [slice(0, HALF), slice(HALF, P)]
+
+        def load_b(queue, h):
+            queue.dma_start(
+                out=b_raw[halves[h]],
+                in_=bb[:, 256 * h : 256 * (h + 1)].rearrange("(p j) m -> p j m", j=PACK),
+            )
+
+        b_raw = sbuf("b_raw", [P, PACK, 256], F32)
+        a_raw = [load("a_raw%d" % c, a, c, 0, R) for c in range(2)]
+        x_raw = [[load("x_raw%d_%d" % (q, c), x, c, 256 * q, 256 * (q + 1)) for c in range(2)] for q in range(2)]
+        load_b(nc.sync, 0)
+        load_b(nc.sync, 1)
+        w0_raw = load("w0_raw", w, 0, 0, M)
+        w1_raw = [load("w1_raw%d" % u, w, 1, 256 * u, 256 * (u + 1)) for u in range(2)]
+
+        a_op = [operand("a_op%d" % c, A_WORDS) for c in range(2)]
+        x_op = [operand("x_op%d" % c, N) for c in range(2)]
+        w_op = [operand("w_op%d" % c, M) for c in range(2)]
+        z_op = operand("z_op", N)
+        b_op = operand("b_op", B_WORDS)
+        warm = sbuf("warm", [P, 8], F32)
+        nc.vector.memset(warm[:, 0:1], 0.0)
+        nc.scalar.activation(out=warm[:, 4:5], in_=warm[:, 0:1], func=GELU)
+
+        a_packed = [sbuf("a_packed%d" % c, [P, PACK * R], BF16) for c in range(2)]
+
+        def a_round(c):
+            deal("vector", a_packed[c], a_raw[c], 0, 16)
+            deal("scalar", a_packed[c], a_raw[c], 16, HALF)
+
+        def a_quantize(c):
+            for s in range(PACK):
+                for h in range(2):
+                    quantize(a_op[c], T * s + HALF * h, a_packed[c], HALF * s, HALF * (s + 1))
+
+        def shared(packed, raw, t, share):
+            if share > 0:
+                interleave("vector", packed, raw, T * t, T * t + share)
+            if share < T:
+                interleave("scalar", packed, raw, T * t + share, T * (t + 1))
+
+        x_packed = [[sbuf("x_packed%d_%d" % (q, c), [P, PACK * 256], BF16) for c in range(2)] for q in range(2)]
+        w1_packed = [sbuf("w1_packed%d" % u, [P, PACK * 256], BF16) for u in range(2)]
+        w0_packed = sbuf("w0_packed", [P, PACK * M], BF16)
+        b_packed = sbuf("b_packed", [P, PACK * 256], BF16)
+
+        def x_round(q, c, s0, s1):
+            shared(x_packed[q][c], x_raw[q][c], 0, s0)
+            shared(x_packed[q][c], x_raw[q][c], 1, s1)
+
+        def x_quantize(q, c, t):
+            quantize(x_op[c], 256 * q + T * t, x_packed[q][c], T * t, T * (t + 1))
+
+        def w_round(c, t, share):
+            if c == 0:
+                shared(w0_packed, w0_raw, t, share)
+            else:
+                shared(w1_packed[t // 2], w1_raw[t // 2], t % 2, share)
+
+        def w_quantize(c, t):
+            if c == 0:
+                quantize(w_op[0], T * t, w0_packed, T * t, T * (t + 1))
+            else:
+                quantize(w_op[1], T * t, w1_packed[t // 2], T * (t % 2), T * (t % 2 + 1))
+
+        banks = [ps.tile([P, 4 * T], F32, name="whole%d" % i) for i in range(4)]
+        y2_banks = [[ps.tile([P, 4 * T], F32, name="rows%d_%d" % (h, q)) for q in range(2)] for h in range(2)]
+
+        def z_products(i):
+            for s in range(PACK):
+                for c in range(2):
+                    product(banks[i][:, T * s : T * (s + 1)], a_op[c], T * s, x_op[c], T * i, whole, c == 0, c == 1)
+
+        z_packed = [sbuf("z_packed%d" % i, [P, PACK * T], BF16) for i in range(4)]
+
+        def z_out(i):
+            nc.scalar.copy(
+                out=z_packed[i][:].rearrange("p (n s) -> p n s", s=PACK),
+                in_=banks[i][:].rearrange("p (s n) -> p n s", s=PACK),
+            )
+
+        def z_quantize(i):
+            quantize(z_op, T * i, z_packed[i], 0, T)
+
+        def y2_products(i):
+            for tt in range(2):
+                for h in range(2):
+                    col = T * (2 * tt + i % 2)
+                    product(y2_banks[h][i // 2][:, col : col + T], b_op, T * tt, z_op, T * i, halves[h], True, True)
+
+        y2 = [sbuf("y2_%d" % h, [P, 2 * N], F32) for h in range(2)]
+
+        def y2_out(engine, h, q):
+            dst = y2[h][:].rearrange("p (t q n) -> p t q n", q=2, n=256)[:, :, q, :]
+            copy(engine, dst, y2_banks[h][q][:].rearrange("p (t n) -> p t n", n=256))
+
+        def y1_products(t, bank, n0, n1):
+            for n in range(n0, n1):
+                for c in range(2):
+                    product(
+                        bank[:, T * n : T * (n + 1)], w_op[c], T * t, x_op[c], T * n, whole, c == 0, c == 1
+                    )
+
+        y = sbuf("y", [P, 4 * N], F32)
+        res = sbuf("res", [P, 4 * N], F32)
+
+        def add(t, bank, n0, n1):
+            cols = slice(T * n0, T * n1)
+            mine = slice(N * t + T * n0, N * t + T * n1)
+            low = slice(N * (t % 2) + T * n0, N * (t % 2) + T * n1)
+            nc.vector.tensor_tensor(out=y[:, mine], in0=bank[:, cols], in1=y2[t // 2][:, low], op=ADD)
+
+        def finish(t, n0, n1):
+            mine = slice(N * t + T * n0, N * t + T * n1)
+            nc.scalar.activation(out=res[:, mine], in_=y[:, mine], func=GELU)
+            nc.sync.dma_start(out=out[T * t : T * (t + 1), T * n0 : T * n1], in_=res[:, mine])
+
+        a_round(0)
+        a_quantize(0)
+        a_round(1)
+        x_round(0, 0, 128, 64)
+        a_quantize(1)
+        x_quantize(0, 0, 0)
+        x_round(0, 1, 64, 0)
+        x_quantize(0, 0, 1)
+        x_quantize(0, 1, 0)
+        x_quantize(0, 1, 1)
+        z_products(0)
+        z_products(1)
+        x_round(1, 0, 64, 64)
+        x_quantize(1, 0, 0)
+        x_quantize(1, 0, 1)
+        x_round(1, 1, 64, 64)
+        x_quantize(1, 1, 0)
+        x_quantize(1, 1, 1)
+        z_out(0)
+        z_products(2)
+        z_products(3)
+        interleave("vector", b_packed, b_raw, 0, 128)
+        interleave("vector", b_packed, b_raw, 128, 256)
+        z_quantize(0)
+        z_out(1)
+        quantize(b_op, 0, b_packed, 0, 256)
+        z_quantize(1)
+        z_out(2)
+        y2_products(0)
+        y2_products(1)
+        z_out(3)
+        z_quantize(2)
+        y2_products(2)
+        w_round(0, 0, 128)
+        z_quantize(3)
+        y2_products(3)
+        y2_out("scalar", 0, 0)
+        w_round(0, 1, 128)
+        w_quantize(0, 0)
+        w_round(0, 2, 128)
+        w_quantize(0, 1)
+        w_round(1, 0, 128)
+        w_round(1, 1, 64)
+        w_quantize(1, 0)
+        w_quantize(0, 2)
+        w_quantize(1, 1)
+        y2_out("scalar", 0, 1)
+        w_round(0, 3, 0)
+        y1_products(0, banks[0], 0, 4)
+        y1_products(1, banks[1], 0, 4)
+        w_round(1, 2, 128)
+        w_round(1, 3, 128)
+        w_quantize(1, 2)
+        w_quantize(0, 3)
+        w_quantize(1, 3)
+        y2_out("scalar", 1, 0)
+        y1_products(2, banks[2], 0, 4)
+        y1_products(3, banks[3], 0, 2)
+        add(0, banks[0], 0, 4)
+        y2_out("scalar", 1, 1)
+        finish(0, 0, 4)
+        y1_products(3, banks[0], 2, 4)
+        add(1, banks[1], 0, 4)
+        finish(1, 0, 4)
+        add(2, banks[2], 0, 4)
+        finish(2, 0, 4)
+        add(3, banks[3], 0, 2)
+        finish(3, 0, 2)
+        add(3, banks[0], 2, 4)
+        finish(3, 2, 4)

@@ -86,12 +86,25 @@ def tile_rows_lora_gelu_kernel(tc, x, w, a, bb, out):
             )
 
         b_raw = sbuf("b_raw", [P, PACK, 256], F32)
-        a_raw = [load("a_raw%d" % c, a, c, 0, R) for c in range(2)]
-        x_raw = [[load("x_raw%d_%d" % (q, c), x, c, 256 * q, 256 * (q + 1)) for c in range(2)] for q in range(2)]
+        a_raw = {}
+        raws = {}
+
+        def load_a(c):
+            a_raw[c] = load("a_raw%d" % c, a, c, 0, R)
+
+        def load_tiles(name, src, c, t0, t1):
+            raw = load("%s_raw%d_%d" % (name, c, t0), src, c, T * t0, T * t1)
+            for t in range(t0, t1):
+                raws[name, c, t] = (raw, T * (t - t0))
+
+        load_a(0)
+        load_tiles("x", x, 0, 0, 4)
+        load_a(1)
+        load_tiles("x", x, 1, 0, 4)
         load_b(nc.sync, 0)
-        load_b(nc.sync, 1)
-        w0_raw = load("w0_raw", w, 0, 0, M)
-        w1_raw = [load("w1_raw%d" % u, w, 1, 256 * u, 256 * (u + 1)) for u in range(2)]
+        load_tiles("w", w, 0, 0, 4)
+        load_tiles("w", w, 1, 0, 2)
+        load_tiles("w", w, 1, 2, 4)
 
         a_op = [operand("a_op%d" % c, A_WORDS) for c in range(2)]
         x_op = [operand("x_op%d" % c, N) for c in range(2)]
@@ -105,43 +118,33 @@ def tile_rows_lora_gelu_kernel(tc, x, w, a, bb, out):
         a_packed = [sbuf("a_packed%d" % c, [P, PACK * R], BF16) for c in range(2)]
 
         def a_round(c):
-            deal("vector", a_packed[c], a_raw[c], 0, 16)
-            deal("scalar", a_packed[c], a_raw[c], 16, HALF)
+            deal("vector", a_packed[c], a_raw[c], 0, 32)
+            deal("scalar", a_packed[c], a_raw[c], 32, HALF)
 
         def a_quantize(c):
             for s in range(PACK):
                 for h in range(2):
                     quantize(a_op[c], T * s + HALF * h, a_packed[c], HALF * s, HALF * (s + 1))
 
-        def shared(packed, raw, t, share):
-            if share > 0:
-                interleave("vector", packed, raw, T * t, T * t + share)
-            if share < T:
-                interleave("scalar", packed, raw, T * t + share, T * (t + 1))
-
-        x_packed = [[sbuf("x_packed%d_%d" % (q, c), [P, PACK * 256], BF16) for c in range(2)] for q in range(2)]
-        w1_packed = [sbuf("w1_packed%d" % u, [P, PACK * 256], BF16) for u in range(2)]
-        w0_packed = sbuf("w0_packed", [P, PACK * M], BF16)
+        packs = {(n, c): sbuf("%s_packed%d" % (n, c), [P, PACK * N], BF16) for n in ("x", "w") for c in range(2)}
+        ops = {"x": x_op, "w": w_op}
         b_packed = sbuf("b_packed", [P, PACK * 256], BF16)
 
-        def x_round(q, c, s0, s1):
-            shared(x_packed[q][c], x_raw[q][c], 0, s0)
-            shared(x_packed[q][c], x_raw[q][c], 1, s1)
+        def rounded(engine, name, c, c0, c1):
+            raw, off = raws[name, c, c0 // T]
+            r0 = off + c0 % T
+            dst = packs[name, c][:, PACK * c0 : PACK * c1].rearrange("p (c i j) -> p c j i", i=4, j=PACK)
+            src = raw[:, :, r0 : r0 + c1 - c0].rearrange("p j (c i) -> p c j i", i=4)
+            copy(engine, dst, src)
 
-        def x_quantize(q, c, t):
-            quantize(x_op[c], 256 * q + T * t, x_packed[q][c], T * t, T * (t + 1))
+        def rnd(name, c, t, share):
+            if share > 0:
+                rounded("vector", name, c, T * t, T * t + share)
+            if share < T:
+                rounded("scalar", name, c, T * t + share, T * (t + 1))
 
-        def w_round(c, t, share):
-            if c == 0:
-                shared(w0_packed, w0_raw, t, share)
-            else:
-                shared(w1_packed[t // 2], w1_raw[t // 2], t % 2, share)
-
-        def w_quantize(c, t):
-            if c == 0:
-                quantize(w_op[0], T * t, w0_packed, T * t, T * (t + 1))
-            else:
-                quantize(w_op[1], T * t, w1_packed[t // 2], T * (t % 2), T * (t % 2 + 1))
+        def qnt(name, c, t0, t1):
+            quantize(ops[name][c], T * t0, packs[name, c], T * t0, T * t1)
 
         banks = [ps.tile([P, 4 * T], F32, name="whole%d" % i) for i in range(4)]
         y2_banks = [[ps.tile([P, 4 * T], F32, name="rows%d_%d" % (h, q)) for q in range(2)] for h in range(2)]
@@ -192,71 +195,72 @@ def tile_rows_lora_gelu_kernel(tc, x, w, a, bb, out):
 
         def finish(t, n0, n1):
             mine = slice(N * t + T * n0, N * t + T * n1)
-            nc.scalar.activation(out=res[:, mine], in_=y[:, mine], func=GELU)
+            nc.scalar.activation(out=res[:, mine], in_=y[:, mine], func=GELU, bias=warm[:, 4:5])
             nc.sync.dma_start(out=out[T * t : T * (t + 1), T * n0 : T * n1], in_=res[:, mine])
 
         a_round(0)
         a_quantize(0)
+        rounded("vector", "x", 0, 0, 256)
+        rounded("scalar", "x", 0, 256, 512)
+        load_b(nc.scalar, 1)
+        qnt("x", 0, 0, 2)
         a_round(1)
-        x_round(0, 0, 128, 64)
+        qnt("x", 0, 2, 4)
         a_quantize(1)
-        x_quantize(0, 0, 0)
-        x_round(0, 1, 64, 0)
-        x_quantize(0, 0, 1)
-        x_quantize(0, 1, 0)
-        x_quantize(0, 1, 1)
+
+        rnd("x", 1, 0, 64)
+        rnd("x", 1, 1, 128)
+        qnt("x", 1, 0, 1)
         z_products(0)
+        rnd("x", 1, 2, 64)
+        qnt("x", 1, 1, 2)
         z_products(1)
-        x_round(1, 0, 64, 64)
-        x_quantize(1, 0, 0)
-        x_quantize(1, 0, 1)
-        x_round(1, 1, 64, 64)
-        x_quantize(1, 1, 0)
-        x_quantize(1, 1, 1)
-        z_out(0)
+        rnd("x", 1, 3, 64)
+        qnt("x", 1, 2, 3)
+        qnt("x", 1, 3, 4)
         z_products(2)
         z_products(3)
         interleave("vector", b_packed, b_raw, 0, 128)
         interleave("vector", b_packed, b_raw, 128, 256)
+        z_out(0)
         z_quantize(0)
-        z_out(1)
         quantize(b_op, 0, b_packed, 0, 256)
-        z_quantize(1)
-        z_out(2)
         y2_products(0)
+        z_out(1)
+        z_quantize(1)
         y2_products(1)
-        z_out(3)
+        z_out(2)
+        rnd("w", 0, 0, 128)
         z_quantize(2)
         y2_products(2)
-        w_round(0, 0, 128)
+        z_out(3)
+        rnd("w", 0, 1, 128)
         z_quantize(3)
         y2_products(3)
         y2_out("scalar", 0, 0)
-        w_round(0, 1, 128)
-        w_quantize(0, 0)
-        w_round(0, 2, 128)
-        w_quantize(0, 1)
-        w_round(1, 0, 128)
-        w_round(1, 1, 64)
-        w_quantize(1, 0)
-        w_quantize(0, 2)
-        w_quantize(1, 1)
-        y2_out("scalar", 0, 1)
-        w_round(0, 3, 0)
-        y1_products(0, banks[0], 0, 4)
-        y1_products(1, banks[1], 0, 4)
-        w_round(1, 2, 128)
-        w_round(1, 3, 128)
-        w_quantize(1, 2)
-        w_quantize(0, 3)
-        w_quantize(1, 3)
+        qnt("w", 0, 0, 2)
         y2_out("scalar", 1, 0)
-        y1_products(2, banks[2], 0, 4)
-        y1_products(3, banks[3], 0, 2)
-        add(0, banks[0], 0, 4)
+        rnd("w", 1, 0, 128)
+        rnd("w", 1, 1, 128)
+        qnt("w", 1, 0, 1)
+        y1_products(0, banks[0], 0, 4)
+        y2_out("scalar", 0, 1)
+        rnd("w", 0, 2, 128)
+        qnt("w", 1, 1, 2)
+        y1_products(1, banks[1], 0, 4)
         y2_out("scalar", 1, 1)
-        finish(0, 0, 4)
+        rnd("w", 0, 3, 0)
+        rnd("w", 1, 2, 128)
+        qnt("w", 0, 2, 3)
+        rnd("w", 1, 3, 0)
+        qnt("w", 0, 3, 4)
+        qnt("w", 1, 2, 3)
+        y1_products(2, banks[2], 0, 4)
+        add(0, banks[0], 0, 4)
+        qnt("w", 1, 3, 4)
+        y1_products(3, banks[3], 0, 2)
         y1_products(3, banks[0], 2, 4)
+        finish(0, 0, 4)
         add(1, banks[1], 0, 4)
         finish(1, 0, 4)
         add(2, banks[2], 0, 4)

from contextlib import ExitStack

import concourse.mybir as mybir

K, R, M, N = 1024, 256, 512, 512
FLOPS = 2 * N * (K * R + K * M + R * M)

F32 = mybir.dt.float32
BF16 = mybir.dt.bfloat16
I32 = mybir.dt.int32
U8 = mybir.dt.uint8
FP8X4 = mybir.dt.float8_e4m3fn_x4
GELU = mybir.ActivationFunctionType.Gelu_apprx_tanh
ADD = mybir.AluOpType.add

P = 128
HALF = 64
PACK = 4
T = 128
PASS = P * PACK
A_WORDS = 8 * HALF
B_WORDS = 2 * T


def tile_rows_lora_gelu_kernel(tc, x, w, a, bb, out):
    nc = tc.nc
    with ExitStack() as ctx:
        sb = ctx.enter_context(tc.tile_pool(name="sb", bufs=1))
        ps = ctx.enter_context(tc.psum_pool(name="ps", bufs=1))
        ctx.enter_context(tc.manual_schedule())

        def sbuf(name, shape, dtype):
            return sb.tile(shape, dtype, name=name, align_bytes=64)

        def load(name, src, c, c0, c1):
            raw = sbuf(name, [P, PACK, c1 - c0], F32)
            rows = src[c * PASS : (c + 1) * PASS, c0:c1]
            nc.sync.dma_start(out=raw[:], in_=rows.rearrange("(p j) n -> p j n", j=PACK))
            return raw

        def copy(engine, dst, src):
            if engine == "vector":
                nc.vector.tensor_copy(out=dst, in_=src)
            else:
                nc.scalar.copy(out=dst, in_=src)

        def interleave(engine, packed, raw, c0, c1):
            dst = packed[:, PACK * c0 : PACK * c1].rearrange("p (c i j) -> p c j i", i=4, j=PACK)
            src = raw[:, :, c0:c1].rearrange("p j (c i) -> p c j i", i=4)
            copy(engine, dst, src)

        def deal(engine, packed, raw, m0, m1):
            dst = packed[:].rearrange("p (s m j) -> p m j s", s=PACK, j=PACK)[:, m0:m1]
            src = raw[:].rearrange("p j (m s) -> p m j s", s=PACK)[:, m0:m1]
            copy(engine, dst, src)

        def operand(name, words):
            both = sbuf(name, [P, words + words // 4], I32)
            return both, both[:, 0:words].bitcast(FP8X4), both[:, words:].bitcast(U8)

        def quantize(op, w0, packed, c0, c1):
            nc.vector.quantize_mx(
                out=op[1][:, w0 : w0 + c1 - c0],
                scales=op[2][:, w0 : w0 + c1 - c0],
                in_=packed[:, PACK * c0 : PACK * c1],
            )

        def product(dst, lhs, l0, rhs, r0, rows, start, stop):
            nc.tensor.matmul_mx(
                out=dst,
                lhsT=lhs[1][rows, l0 : l0 + T],
                lhsT_scale=lhs[2][rows, l0 : l0 + T],
                rhs=rhs[1][rows, r0 : r0 + T],
                rhs_scale=rhs[2][rows, r0 : r0 + T],
                start=start,
                stop=stop,
            )

        whole = slice(0, P)
        halves = [slice(0, HALF), slice(HALF, P)]

        def load_b(queue, h):
            queue.dma_start(
                out=b_raw[halves[h]],
                in_=bb[:, 256 * h : 256 * (h + 1)].rearrange("(p j) m -> p j m", j=PACK),
            )

        b_raw = sbuf("b_raw", [P, PACK, 256], F32)
        a_raw = {}
        raws = {}

        def load_a(c):
            a_raw[c] = load("a_raw%d" % c, a, c, 0, R)

        def load_tiles(name, src, c, t0, t1):
            raw = load("%s_raw%d_%d" % (name, c, t0), src, c, T * t0, T * t1)
            for t in range(t0, t1):
                raws[name, c, t] = (raw, T * (t - t0))

        load_a(0)
        load_tiles("x", x, 0, 0, 4)
        load_a(1)
        load_tiles("x", x, 1, 0, 4)
        load_b(nc.sync, 0)
        load_tiles("w", w, 0, 0, 4)
        load_tiles("w", w, 1, 0, 2)
        load_tiles("w", w, 1, 2, 4)

        a_op = [operand("a_op%d" % c, A_WORDS) for c in range(2)]
        x_op = [operand("x_op%d" % c, N) for c in range(2)]
        w_op = [operand("w_op%d" % c, M) for c in range(2)]
        z_op = operand("z_op", N)
        b_op = operand("b_op", B_WORDS)
        warm = sbuf("warm", [P, 8], F32)
        nc.vector.memset(warm[:, 0:1], 0.0)
        nc.scalar.activation(out=warm[:, 4:5], in_=warm[:, 0:1], func=GELU)

        a_packed = [sbuf("a_packed%d" % c, [P, PACK * R], BF16) for c in range(2)]

        def a_round(c):
            deal("vector", a_packed[c], a_raw[c], 0, 32)
            deal("scalar", a_packed[c], a_raw[c], 32, HALF)

        def a_quantize(c):
            for s in range(PACK):
                for h in range(2):
                    quantize(a_op[c], T * s + HALF * h, a_packed[c], HALF * s, HALF * (s + 1))

        packs = {(n, c): sbuf("%s_packed%d" % (n, c), [P, PACK * N], BF16) for n in ("x", "w") for c in range(2)}
        ops = {"x": x_op, "w": w_op}
        b_packed = sbuf("b_packed", [P, PACK * 256], BF16)

        def rounded(engine, name, c, c0, c1):
            raw, off = raws[name, c, c0 // T]
            r0 = off + c0 % T
            dst = packs[name, c][:, PACK * c0 : PACK * c1].rearrange("p (c i j) -> p c j i", i=4, j=PACK)
            src = raw[:, :, r0 : r0 + c1 - c0].rearrange("p j (c i) -> p c j i", i=4)
            copy(engine, dst, src)

        def rnd(name, c, t, share):
            if share > 0:
                rounded("vector", name, c, T * t, T * t + share)
            if share < T:
                rounded("scalar", name, c, T * t + share, T * (t + 1))

        def qnt(name, c, t0, t1):
            quantize(ops[name][c], T * t0, packs[name, c], T * t0, T * t1)

        banks = [ps.tile([P, 4 * T], F32, name="whole%d" % i) for i in range(4)]
        y2_banks = [[ps.tile([P, 4 * T], F32, name="rows%d_%d" % (h, q)) for q in range(2)] for h in range(2)]

        def z_products(i):
            for s in range(PACK):
                for c in range(2):
                    product(banks[i][:, T * s : T * (s + 1)], a_op[c], T * s, x_op[c], T * i, whole, c == 0, c == 1)

        z_packed = [sbuf("z_packed%d" % i, [P, PACK * T], BF16) for i in range(4)]

        def z_out(i):
            nc.scalar.copy(
                out=z_packed[i][:].rearrange("p (n s) -> p n s", s=PACK),
                in_=banks[i][:].rearrange("p (s n) -> p n s", s=PACK),
            )

        def z_quantize(i):
            quantize(z_op, T * i, z_packed[i], 0, T)

        def y2_products(i):
            for tt in range(2):
                for h in range(2):
                    col = T * (2 * tt + i % 2)
                    product(y2_banks[h][i // 2][:, col : col + T], b_op, T * tt, z_op, T * i, halves[h], True, True)

        y2 = [sbuf("y2_%d" % h, [P, 2 * N], F32) for h in range(2)]

        def y2_out(engine, h, q):
            dst = y2[h][:].rearrange("p (t q n) -> p t q n", q=2, n=256)[:, :, q, :]
            copy(engine, dst, y2_banks[h][q][:].rearrange("p (t n) -> p t n", n=256))

        def y1_products(t, bank, n0, n1):
            for n in range(n0, n1):
                for c in range(2):
                    product(
                        bank[:, T * n : T * (n + 1)], w_op[c], T * t, x_op[c], T * n, whole, c == 0, c == 1
                    )

        y = sbuf("y", [P, 4 * N], F32)
        res = sbuf("res", [P, 4 * N], F32)

        def add(t, bank, n0, n1):
            cols = slice(T * n0, T * n1)
            mine = slice(N * t + T * n0, N * t + T * n1)
            low = slice(N * (t % 2) + T * n0, N * (t % 2) + T * n1)
            nc.vector.tensor_tensor(out=y[:, mine], in0=bank[:, cols], in1=y2[t // 2][:, low], op=ADD)

        def finish(t, n0, n1):
            mine = slice(N * t + T * n0, N * t + T * n1)
            nc.scalar.activation(out=res[:, mine], in_=y[:, mine], func=GELU, bias=warm[:, 4:5])
            nc.sync.dma_start(out=out[T * t : T * (t + 1), T * n0 : T * n1], in_=res[:, mine])

        a_round(0)
        a_quantize(0)
        rounded("vector", "x", 0, 0, 256)
        rounded("scalar", "x", 0, 256, 512)
        load_b(nc.scalar, 1)
        qnt("x", 0, 0, 2)
        a_round(1)
        qnt("x", 0, 2, 4)
        a_quantize(1)

        rnd("x", 1, 0, 64)
        rnd("x", 1, 1, 128)
        qnt("x", 1, 0, 1)
        z_products(0)
        rnd("x", 1, 2, 64)
        qnt("x", 1, 1, 2)
        z_products(1)
        rnd("x", 1, 3, 64)
        qnt("x", 1, 2, 3)
        qnt("x", 1, 3, 4)
        z_products(2)
        z_products(3)
        interleave("vector", b_packed, b_raw, 0, 128)
        interleave("vector", b_packed, b_raw, 128, 256)
        z_out(0)
        z_quantize(0)
        quantize(b_op, 0, b_packed, 0, 256)
        y2_products(0)
        z_out(1)
        z_quantize(1)
        y2_products(1)
        z_out(2)
        rnd("w", 0, 0, 128)
        z_quantize(2)
        y2_products(2)
        z_out(3)
        rnd("w", 0, 1, 128)
        z_quantize(3)
        y2_products(3)
        y2_out("scalar", 0, 0)
        qnt("w", 0, 0, 2)
        y2_out("scalar", 1, 0)
        rnd("w", 1, 0, 128)
        rnd("w", 1, 1, 128)
        qnt("w", 1, 0, 1)
        y1_products(0, banks[0], 0, 4)
        y2_out("scalar", 0, 1)
        rnd("w", 0, 2, 128)
        qnt("w", 1, 1, 2)
        y1_products(1, banks[1], 0, 4)
        y2_out("scalar", 1, 1)
        rnd("w", 0, 3, 0)
        rnd("w", 1, 2, 128)
        qnt("w", 0, 2, 3)
        rnd("w", 1, 3, 0)
        qnt("w", 0, 3, 4)
        qnt("w", 1, 2, 3)
        y1_products(2, banks[2], 0, 4)
        add(0, banks[0], 0, 4)
        qnt("w", 1, 3, 4)
        y1_products(3, banks[3], 0, 2)
        y1_products(3, banks[0], 2, 4)
        finish(0, 0, 4)
        add(1, banks[1], 0, 4)
        finish(1, 0, 4)
        add(2, banks[2], 0, 4)
        finish(2, 0, 4)
        add(3, banks[3], 0, 2)
        finish(3, 0, 2)
        add(3, banks[0], 2, 4)
        finish(3, 2, 4)
